import numpy as np
import ml_dtypes


def mxq(x, axis, fmt="e4m3"):
    dtype, down = {"e4m3": (ml_dtypes.float8_e4m3fn, 7), "e5m2": (ml_dtypes.float8_e5m2, 14)}[fmt]
    v = np.moveaxis(np.asarray(x, np.float32).astype(ml_dtypes.bfloat16).astype(np.float64), axis, -1)
    blocks = v.reshape(v.shape[:-1] + (-1, 32))
    amax = np.abs(blocks).max(-1, keepdims=True)
    byte = np.maximum(np.where(amax > 0, np.frexp(amax)[1] - 1 + 127, 0) - down, 1)
    scale = np.exp2(byte - 127.0)
    codes = (blocks / scale).astype(np.float32).astype(dtype).astype(np.float64)
    return np.moveaxis((codes * scale).reshape(v.shape), -1, axis)


WIDE = False


def mx_kscale(k):
    if not WIDE:
        return np.ones(k)
    levels = np.array([30, -30])
    if k % 512:
        return np.exp2(np.random.permutation(np.resize(levels, k // 32))).repeat(32)
    a = np.empty((k // 512, 16))
    for p in range(k // 512):
        a[p, :8] = np.random.permutation(np.resize(levels, 8))
        for g in range(8):
            far = levels[np.abs(levels - a[p, g]) >= 10]
            a[p, g + 8] = far[np.random.randint(len(far))]
    return np.exp2(a.ravel()).repeat(32)


def f64(x):
    return np.asarray(x).astype(np.float64)


def striped(idx):
    return np.tile(np.asarray(idx).reshape(-1, 16).T, (8, 1)).astype(np.uint16)


def unstriped(offs):
    return offs[:16].T.reshape(-1).astype(np.int64)


E2M1 = np.array([0.0, 0.5, 1.0, 1.5, 2.0, 3.0, 4.0, 6.0, -0.0, -0.5, -1.0, -1.5, -2.0, -3.0, -4.0, -6.0])


def pack_weight(w, fmt):
    k, n = w.shape
    w = f64(np.asarray(w, np.float32).astype(ml_dtypes.bfloat16)).reshape(k // 32, 32, n)
    amax = np.abs(w).max(1)
    if fmt in ("e4m3", "e5m2"):
        byte = np.frexp(amax)[1] - 1 + 127 - (7 if fmt == "e4m3" else 14)
    else:
        mant, ex = np.frexp(amax / 6.0)
        byte = np.where(mant > 0.5, ex, ex - 1) + 127
    byte = np.clip(np.where(amax > 0, byte, 1), 1, 254)
    scaled = (w * np.exp2(127.0 - byte)[:, None, :]).reshape(k, n).astype(np.float32)
    by_word = np.ascontiguousarray(scaled.reshape(k // 512, 128, 4, n).transpose(0, 1, 3, 2))
    if fmt in ("e4m3", "e5m2"):
        words = by_word.astype(ml_dtypes.float8_e4m3fn if fmt == "e4m3" else ml_dtypes.float8_e5m2).view(np.uint8)
    else:
        c = by_word.astype(ml_dtypes.float4_e2m1fn).view(np.uint8) & 0xF
        words = (c[..., 0::2] | (c[..., 1::2] << 4)).reshape(k // 512, 128, 2 * n)
    return np.ascontiguousarray(words), np.ascontiguousarray(byte.astype(np.uint8).reshape(k // 512, 16, n))


def unpack_weight(words, scales, fmt):
    g, _, n = scales.shape
    words = np.ascontiguousarray(words).reshape(g, 128, n, -1)
    if fmt in ("e4m3", "e5m2"):
        vals = words.view(ml_dtypes.float8_e4m3fn if fmt == "e4m3" else ml_dtypes.float8_e5m2).astype(np.float64)
    else:
        nib = np.empty((g, 128, n, 4), np.uint8)
        nib[..., 0::2] = words & 0xF
        nib[..., 1::2] = words >> 4
        vals = E2M1[nib]
    vals = vals * np.repeat(np.exp2(scales.astype(np.float64) - 127.0), 8, axis=1)[..., None]
    return vals.transpose(0, 1, 3, 2).reshape(g * 512, n)


def sigmoid(v):
    return 1.0 / (1.0 + np.exp(-v))


K, F, T, Z, J, R, O, N, E = 512, 512, 1024, 1024, 256, 512, 128, 256, 1024


def setup_inputs():
    n = np.random.standard_normal
    idx = np.random.permutation(T)[:J]
    idx2 = np.random.permutation(Z)[:J]
    idx3 = np.random.permutation(J)[:J]
    idx4 = np.random.permutation(J)[:O]
    idx5 = np.random.permutation(J)[:O]
    idx6 = np.random.permutation(E)[:O]
    fk = mx_kscale(K)
    ff = mx_kscale(F)
    fr = mx_kscale(R)
    xtp = pack_weight(n((K, T)) / fk[:, None], "e4m3")
    wp = pack_weight(n((K, R)) * 1 / np.sqrt(K) * fk[:, None], "e2m1")
    xop = pack_weight(n((F, Z)) / ff[:, None], "e2m1")
    w2p = pack_weight(n((F, R)) * 1 / np.sqrt(F) * ff[:, None] * fr, "e5m2")
    wbp = pack_weight(n((R, N)) * 1 / np.sqrt(R) / fr[:, None], "e5m2")
    return {
        "xt_words": xtp[0],
        "xt_scales": xtp[1],
        "w_words": wp[0],
        "w_scales": wp[1],
        "xo_words": xop[0],
        "xo_scales": xop[1],
        "w2_words": w2p[0],
        "w2_scales": w2p[1],
        "sg": (np.random.uniform(0.6, 1.6, (R, 1))).astype(np.float32),
        "bg": (np.random.uniform(-1.0, 1.0, (R, 1))).astype(np.float32),
        "wb_words": wbp[0],
        "wb_scales": wbp[1],
        "tz": (n((N, E))).astype(np.float32),
        "offs": striped(idx),
        "offs2": striped(idx2),
        "offs3": striped(idx3),
        "offs4": striped(idx4),
        "offs5": striped(idx5),
        "offs6": striped(idx6),
    }


def reference(xt_words, xt_scales, w_words, w_scales, xo_words, xo_scales, w2_words, w2_scales, sg, bg, wb_words, wb_scales, tz, offs, offs2, offs3, offs4, offs5, offs6):
    idx = unstriped(offs)
    idx2 = unstriped(offs2)
    idx3 = unstriped(offs3)
    idx4 = unstriped(offs4)
    idx5 = unstriped(offs5)
    idx6 = unstriped(offs6)
    xtu = unpack_weight(xt_words, xt_scales, "e4m3")
    wu = unpack_weight(w_words, w_scales, "e2m1")
    xou = unpack_weight(xo_words, xo_scales, "e2m1")
    w2u = unpack_weight(w2_words, w2_scales, "e5m2")
    wbu = unpack_weight(wb_words, wb_scales, "e5m2")
    xtidxg = xtu[:, idx]
    a = wu.T @ xtidxg
    xoidx2g = xou[:, idx2]
    b = w2u.T @ xoidx2g
    hg = b * sigmoid(a[:, idx3] * f64(sg) + f64(bg))
    hid = np.maximum(hg[:, idx4], hg[:, idx5])
    hidq = mxq(hid, 0, "e4m3")
    p = wbu.T @ hidq
    y = p + f64(tz)[:, idx6]
    return y

@@ -1,0 +1,180 @@
+from contextlib import ExitStack
+
+import concourse.mybir as mybir
+
+FLOPS = 301989888
+
+F32 = mybir.dt.float32
+BF16 = mybir.dt.bfloat16
+I32 = mybir.dt.int32
+U32 = mybir.dt.uint32
+U16 = mybir.dt.uint16
+U8 = mybir.dt.uint8
+E4M3 = mybir.dt.float8_e4m3fn_x4
+E5M2 = mybir.dt.float8_e5m2_x4
+E2M1 = mybir.dt.float4_e2m1fn_x4
+ACT = mybir.ActivationFunctionType
+ALU = mybir.AluOpType
+
+P = 128
+PACK = 4
+T = 1024
+J = 256
+R = 512
+O = 128
+N = 256
+E = 1024
+LINE = 16
+
+
+def load_scale_rows(queue, plane, scales):
+    for q in range(4):
+        queue.dma_start(
+            out=plane[32 * q : 32 * q + 4, :].bitcast(I32),
+            in_=scales[0, 4 * q : 4 * q + 4, :].bitcast(I32),
+        )
+
+
+def deal_views(dealt, raw, run):
+    return (
+        dealt[:].rearrange("p t (c i) -> p c t i", i=run),
+        raw.rearrange("p (c i t) -> p c t i", i=run, t=PACK),
+    )
+
+
+def tile_list_gatedtwo_twotab_one_tabled_kernel(
+    tc, xt_words, xt_scales, w_words, w_scales, xo_words, xo_scales, w2_words, w2_scales,
+    sg, bg, wb_words, wb_scales, tz, offs, offs2, offs3, offs4, offs5, offs6, out,
+):
+    nc = tc.nc
+    with ExitStack() as ctx:
+        sb = ctx.enter_context(tc.tile_pool(name="sb", bufs=1))
+        ps = ctx.enter_context(tc.psum_pool(name="ps", bufs=1))
+
+        def tile(name, shape, dtype):
+            return sb.tile(shape, dtype, name=name, align_bytes=64)
+
+        l1 = tile("l1", [P, J // 16], U16)
+        l2 = tile("l2", [P, J // 16], U16)
+        l3 = tile("l3", [P, J // 16], U16)
+        l4 = tile("l4", [P, O // 16], U16)
+        l5 = tile("l5", [P, O // 16], U16)
+        l6 = tile("l6", [P, O // 16], U16)
+
+        xt_w = tile("xt_w", [P, T], I32)
+        xt_s = tile("xt_s", [P, T], U8)
+        xo_w = tile("xo_w", [P, T], U16)
+        xo_s = tile("xo_s", [P, T], U8)
+        w_w = tile("w_w", [P, R], U16)
+        wts_s = tile("wts_s", [P, 2 * R + N], U8)
+        w_s, w2_s, wb_s = wts_s[:, :R], wts_s[:, R : 2 * R], wts_s[:, 2 * R :]
+        w2_w = tile("w2_w", [P, R], I32)
+        wb_w = tile("wb_w", [P, N], I32)
+        sg_t = tile("sg_t", [P, PACK], F32)
+        bg_t = tile("bg_t", [P, PACK], F32)
+        tz_t = tile("tz_t", [P, 2, E], F32)
+
+        nc.vector.memset(xt_s[:].bitcast(I32), 0)
+        nc.gpsimd.memset(wts_s[:].bitcast(I32), 0)
+        nc.vector.memset(xo_s[:].bitcast(I32), 0)
+
+        nc.sync.dma_start(l1[:], offs)
+        nc.sync.dma_start(out=xt_w[:], in_=xt_words[0].rearrange("p n t -> p (n t)").bitcast(I32))
+        load_scale_rows(nc.scalar, xt_s, xt_scales)
+        nc.sync.dma_start(out=w_w[:].bitcast(I32), in_=w_words[0].bitcast(I32))
+        load_scale_rows(nc.sync, w_s, w_scales)
+        nc.sync.dma_start(l2[:], offs2)
+        nc.sync.dma_start(out=xo_w[:].bitcast(I32), in_=xo_words[0].bitcast(I32))
+        load_scale_rows(nc.sync, xo_s, xo_scales)
+        nc.sync.dma_start(l3[:], offs3)
+        nc.sync.dma_start(out=w2_w[:], in_=w2_words[0].rearrange("p n t -> p (n t)").bitcast(I32))
+        load_scale_rows(nc.sync, w2_s, w2_scales)
+        nc.gpsimd.dma_start(out=sg_t[:], in_=sg.rearrange("(p t) o -> p (t o)", t=PACK))
+        nc.gpsimd.dma_start(out=bg_t[:], in_=bg.rearrange("(p t) o -> p (t o)", t=PACK))
+        nc.sync.dma_start(l4[:], offs4)
+        nc.sync.dma_start(l5[:], offs5)
+        nc.sync.dma_start(l6[:], offs6)
+        nc.sync.dma_start(out=wb_w[:], in_=wb_words[0].rearrange("p n t -> p (n t)").bitcast(I32))
+        nc.sync.dma_start(out=tz_t[:], in_=tz.rearrange("(h p) e -> p h e", p=P))
+        load_scale_rows(nc.gpsimd, wb_s, wb_scales)
+
+        xt_wg = tile("xt_wg", [P, J], U32)
+        xt_sg = tile("xt_sg", [P, J], U8)
+        nc.vector.tensor_copy(xt_sg[:], xt_s[:].indirect(l1[:]))
+        nc.vector.tensor_copy(xt_wg[:], xt_w[:].bitcast(U32).indirect(l1[:]))
+        w_wd = tile("w_wd", [P, PACK, P], U16)
+        w_sd = tile("w_sd", [P, PACK, P], U8)
+        nc.scalar.copy(*deal_views(w_wd, w_w[:], LINE // 2))
+        nc.vector.tensor_copy(*deal_views(w_sd, w_s, LINE))
+
+        a_sb = []
+        for t in range(PACK):
+            a_ps = ps.tile([P, J], F32, name="a_ps%d" % t)
+            nc.tensor.matmul_mx(
+                out=a_ps[:], lhsT=w_wd[:, t, :].bitcast(E2M1), lhsT_scale=w_sd[:, t, :],
+                rhs=xt_wg[:].bitcast(E4M3), rhs_scale=xt_sg[:], start=True, stop=True,
+            )
+            a_t = tile("a%d" % t, [P, J], F32)
+            if t < 2:
+                nc.scalar.copy(a_t[:], a_ps[:])
+            else:
+                nc.vector.tensor_copy(a_t[:], a_ps[:])
+            a_sb.append(a_t)
+
+        xo_wg = tile("xo_wg", [P, J], U16)
+        xo_sg = tile("xo_sg", [P, J], U8)
+        nc.vector.tensor_copy(xo_wg[:], xo_w[:].indirect(l2[:]))
+        nc.vector.tensor_copy(xo_sg[:], xo_s[:].indirect(l2[:]))
+        w2_wd = tile("w2_wd", [P, PACK, P], U32)
+        w2_sd = tile("w2_sd", [P, PACK, P], U8)
+        nc.scalar.copy(*deal_views(w2_wd, w2_w[:].bitcast(U32), LINE // 4))
+        nc.vector.tensor_copy(*deal_views(w2_sd, w2_s, LINE))
+
+        b_ps = [ps.tile([P, 2, J], F32, name="b_ps%d" % u) for u in range(2)]
+        for t in range(PACK):
+            nc.tensor.matmul_mx(
+                out=b_ps[t // 2][:, t % 2, :], lhsT=w2_wd[:, t, :].bitcast(E5M2), lhsT_scale=w2_sd[:, t, :],
+                rhs=xo_wg[:].bitcast(E2M1), rhs_scale=xo_sg[:], start=True, stop=True,
+            )
+
+        gate = tile("gate", [P, PACK, J], F32)
+        for t in range(PACK):
+            for u in range(2):
+                nc.scalar.activation(
+                    out=gate[:, t, u * 128 : (u + 1) * 128],
+                    in_=a_sb[t][:].indirect(l3[:, 8 * u : 8 * u + 8]),
+                    func=ACT.Sigmoid, bias=bg_t[:, t : t + 1], scale=sg_t[:, t : t + 1],
+                )
+
+        g4 = tile("g4", [P, PACK, O], F32)
+        g5 = tile("g5", [P, PACK, O], F32)
+        for t in range(PACK):
+            hg = tile("hg%d" % t, [P, J], F32)
+            nc.vector.tensor_tensor(hg[:], gate[:, t, :], b_ps[t // 2][:, t % 2, :], ALU.mult)
+            nc.vector.tensor_copy(g4[:, t, :], hg[:].indirect(l4[:]))
+            nc.scalar.activation(out=g5[:, t, :], in_=hg[:].indirect(l5[:]), func=ACT.Copy)
+
+        tz_g = tile("tz_g", [P, 2, O], F32)
+        for h in range(2):
+            nc.scalar.activation(out=tz_g[:, h, :], in_=tz_t[:, h, :].indirect(l6[:]), func=ACT.Copy)
+
+        hid = tile("hid", [P, O * PACK], BF16)
+        nc.vector.tensor_tensor(
+            hid[:].rearrange("p (c i t) -> p c t i", i=4, t=PACK),
+            g4[:].rearrange("p t (c i) -> p c t i", i=4),
+            g5[:].rearrange("p t (c i) -> p c t i", i=4),
+            ALU.max,
+        )
+        hid_w = tile("hid_w", [P, O], U32)
+        hid_s = tile("hid_s", [P, O], U8)
+        nc.vector.quantize_mx(out=hid_w[:].bitcast(E4M3), scales=hid_s[:], in_=hid[:])
+
+        p_ps = ps.tile([P, 2, O], F32, name="p_ps")
+        for h in range(2):
+            nc.tensor.matmul_mx(
+                out=p_ps[:, h, :], lhsT=wb_w[:, h * P : (h + 1) * P].bitcast(E5M2), lhsT_scale=wb_s[:, h * P : (h + 1) * P],
+                rhs=hid_w[:].bitcast(E4M3), rhs_scale=hid_s[:], start=True, stop=True,
+            )
+        y = tile("y", [P, 2, O], F32)
+        nc.vector.tensor_tensor(y[:], p_ps[:], tz_g[:], ALU.add)
+        nc.sync.dma_start(out=out.rearrange("(h p) o -> p h o", p=P), in_=y[:])

@@ -27,19 +27,19 @@ E = 1024
 LINE = 16
 
 
-def load_scale_rows(queue, plane, scales):
-    for q in range(4):
-        queue.dma_start(
-            out=plane[32 * q : 32 * q + 4, :].bitcast(I32),
-            in_=scales[0, 4 * q : 4 * q + 4, :].bitcast(I32),
-        )
-
-
 def deal_views(dealt, raw, run):
     return (
-        dealt[:].rearrange("p t (c i) -> p c t i", i=run),
+        dealt.rearrange("p (t c i) -> p c t i", i=run, t=PACK),
         raw.rearrange("p (c i t) -> p c t i", i=run, t=PACK),
     )
+
+
+def spread_scale_rows(queue, planes):
+    for q in range(1, 4):
+        queue.dma_start(
+            out=planes[32 * q : 32 * q + 4, :].bitcast(I32),
+            in_=planes[4 * q : 4 * q + 4, :].bitcast(I32),
+        )
 
 
 def tile_list_gatedtwo_twotab_one_tabled_kernel(
@@ -51,8 +51,8 @@ def tile_list_gatedtwo_twotab_one_tabled_kernel(
         sb = ctx.enter_context(tc.tile_pool(name="sb", bufs=1))
         ps = ctx.enter_context(tc.psum_pool(name="ps", bufs=1))
 
-        def tile(name, shape, dtype):
-            return sb.tile(shape, dtype, name=name, align_bytes=64)
+        def tile(name, shape, dtype, tag=None):
+            return sb.tile(shape, dtype, name=name, tag=tag or name, align_bytes=64)
 
         l1 = tile("l1", [P, J // 16], U16)
         l2 = tile("l2", [P, J // 16], U16)
@@ -66,85 +66,88 @@ def tile_list_gatedtwo_twotab_one_tabled_kernel(
         xo_w = tile("xo_w", [P, T], U16)
         xo_s = tile("xo_s", [P, T], U8)
         w_w = tile("w_w", [P, R], U16)
-        wts_s = tile("wts_s", [P, 2 * R + N], U8)
-        w_s, w2_s, wb_s = wts_s[:, :R], wts_s[:, R : 2 * R], wts_s[:, 2 * R :]
         w2_w = tile("w2_w", [P, R], I32)
         wb_w = tile("wb_w", [P, N], I32)
+        raw_s = tile("raw_s", [P, 2 * R], U8)
+        planes_a = tile("planes_a", [P, J + R], U8)
+        planes_b = tile("planes_b", [P, J + R + N], U8)
         sg_t = tile("sg_t", [P, PACK], F32)
         bg_t = tile("bg_t", [P, PACK], F32)
-        tz_t = tile("tz_t", [P, 2, E], F32)
 
-        nc.vector.memset(xt_s[:].bitcast(I32), 0)
-        nc.gpsimd.memset(wts_s[:].bitcast(I32), 0)
+        nc.gpsimd.memset(xt_s[:].bitcast(I32), 0)
+        nc.vector.memset(raw_s[:].bitcast(I32), 0)
         nc.vector.memset(xo_s[:].bitcast(I32), 0)
 
+        def load_rows(queue, dst, scales):
+            queue.dma_start(out=dst.bitcast(I32), in_=scales[0].bitcast(I32))
+
         nc.sync.dma_start(l1[:], offs)
-        nc.sync.dma_start(out=xt_w[:], in_=xt_words[0].rearrange("p n t -> p (n t)").bitcast(I32))
-        load_scale_rows(nc.scalar, xt_s, xt_scales)
-        nc.sync.dma_start(out=w_w[:].bitcast(I32), in_=w_words[0].bitcast(I32))
-        load_scale_rows(nc.sync, w_s, w_scales)
+        nc.sync.dma_start(out=wb_w[:], in_=wb_words[0].rearrange("p n t -> p (n t)").bitcast(I32))
+        load_rows(nc.sync, xt_s[:16, :], xt_scales)
+        load_rows(nc.sync, raw_s[:16, :R], w_scales)
         nc.sync.dma_start(l2[:], offs2)
-        nc.sync.dma_start(out=xo_w[:].bitcast(I32), in_=xo_words[0].bitcast(I32))
-        load_scale_rows(nc.sync, xo_s, xo_scales)
+        load_rows(nc.sync, xo_s[:16, :], xo_scales)
+        load_rows(nc.sync, raw_s[:16, R:], w2_scales)
+        nc.sync.dma_start(out=xt_w[:], in_=xt_words[0].rearrange("p n t -> p (n t)").bitcast(I32))
+        load_rows(nc.gpsimd, planes_b[:16, J + R :], wb_scales)
         nc.sync.dma_start(l3[:], offs3)
+        nc.sync.dma_start(out=sg_t[:], in_=sg.rearrange("(p t) o -> p (t o)", t=PACK))
+        nc.sync.dma_start(out=bg_t[:], in_=bg.rearrange("(p t) o -> p (t o)", t=PACK))
+        nc.sync.dma_start(out=w_w[:].bitcast(I32), in_=w_words[0].bitcast(I32))
+        nc.sync.dma_start(out=xo_w[:].bitcast(I32), in_=xo_words[0].bitcast(I32))
         nc.sync.dma_start(out=w2_w[:], in_=w2_words[0].rearrange("p n t -> p (n t)").bitcast(I32))
-        load_scale_rows(nc.sync, w2_s, w2_scales)
-        nc.gpsimd.dma_start(out=sg_t[:], in_=sg.rearrange("(p t) o -> p (t o)", t=PACK))
-        nc.gpsimd.dma_start(out=bg_t[:], in_=bg.rearrange("(p t) o -> p (t o)", t=PACK))
         nc.sync.dma_start(l4[:], offs4)
         nc.sync.dma_start(l5[:], offs5)
         nc.sync.dma_start(l6[:], offs6)
-        nc.sync.dma_start(out=wb_w[:], in_=wb_words[0].rearrange("p n t -> p (n t)").bitcast(I32))
-        nc.sync.dma_start(out=tz_t[:], in_=tz.rearrange("(h p) e -> p h e", p=P))
-        load_scale_rows(nc.gpsimd, wb_s, wb_scales)
 
-        xt_wg = tile("xt_wg", [P, J], U32)
         xt_sg = tile("xt_sg", [P, J], U8)
         nc.vector.tensor_copy(xt_sg[:], xt_s[:].indirect(l1[:]))
-        nc.vector.tensor_copy(xt_wg[:], xt_w[:].bitcast(U32).indirect(l1[:]))
-        w_wd = tile("w_wd", [P, PACK, P], U16)
-        w_sd = tile("w_sd", [P, PACK, P], U8)
-        nc.scalar.copy(*deal_views(w_wd, w_w[:], LINE // 2))
-        nc.vector.tensor_copy(*deal_views(w_sd, w_s, LINE))
+        nc.vector.tensor_copy(*deal_views(planes_a[:, J:], raw_s[:, :R], LINE))
+        nc.vector.tensor_copy(planes_a[:, :J].bitcast(I32), xt_sg[:].bitcast(I32))
+        spread_scale_rows(nc.sync, planes_a)
 
-        a_sb = []
-        for t in range(PACK):
-            a_ps = ps.tile([P, J], F32, name="a_ps%d" % t)
-            nc.tensor.matmul_mx(
-                out=a_ps[:], lhsT=w_wd[:, t, :].bitcast(E2M1), lhsT_scale=w_sd[:, t, :],
-                rhs=xt_wg[:].bitcast(E4M3), rhs_scale=xt_sg[:], start=True, stop=True,
-            )
-            a_t = tile("a%d" % t, [P, J], F32)
-            if t < 2:
-                nc.scalar.copy(a_t[:], a_ps[:])
-            else:
-                nc.vector.tensor_copy(a_t[:], a_ps[:])
-            a_sb.append(a_t)
-
-        xo_wg = tile("xo_wg", [P, J], U16)
         xo_sg = tile("xo_sg", [P, J], U8)
-        nc.vector.tensor_copy(xo_wg[:], xo_w[:].indirect(l2[:]))
         nc.vector.tensor_copy(xo_sg[:], xo_s[:].indirect(l2[:]))
-        w2_wd = tile("w2_wd", [P, PACK, P], U32)
-        w2_sd = tile("w2_sd", [P, PACK, P], U8)
-        nc.scalar.copy(*deal_views(w2_wd, w2_w[:].bitcast(U32), LINE // 4))
-        nc.vector.tensor_copy(*deal_views(w2_sd, w2_s, LINE))
+        nc.vector.tensor_copy(*deal_views(planes_b[:, J : J + R], raw_s[:, R:], LINE))
+        nc.vector.tensor_copy(planes_b[:, :J].bitcast(I32), xo_sg[:].bitcast(I32))
+        spread_scale_rows(nc.sync, planes_b)
 
+        xt_wg = tile("xt_wg", [P, J], U32)
+        w_wd = tile("w_wd", [P, R], U16)
+        nc.vector.tensor_copy(xt_wg[:], xt_w[:].bitcast(U32).indirect(l1[:]))
+        nc.vector.tensor_copy(*deal_views(w_wd[:], w_w[:], LINE // 2))
+        xo_wg = tile("xo_wg", [P, J], U16)
+        w2_wd = tile("w2_wd", [P, R], I32)
+        nc.vector.tensor_copy(xo_wg[:], xo_w[:].indirect(l2[:]))
+        nc.vector.tensor_copy(*deal_views(w2_wd[:], w2_w[:], LINE // 4))
+
+        tz_sb = [tile("tz%d" % h, [P, E], F32, tag=("xo_w", "w2_w")[h]) for h in range(2)]
+        for h in range(2):
+            nc.sync.dma_start(out=tz_sb[h][:], in_=tz[h * P : (h + 1) * P, :])
+
+        a_ps = [ps.tile([P, J], F32, name="a_ps%d" % t) for t in range(PACK)]
+        for t in range(PACK):
+            cols = slice(t * P, (t + 1) * P)
+            nc.tensor.matmul_mx(
+                out=a_ps[t][:], lhsT=w_wd[:, cols].bitcast(E2M1), lhsT_scale=planes_a[:, J:][:, cols],
+                rhs=xt_wg[:].bitcast(E4M3), rhs_scale=planes_a[:, :J], start=True, stop=True,
+            )
         b_ps = [ps.tile([P, 2, J], F32, name="b_ps%d" % u) for u in range(2)]
         for t in range(PACK):
+            cols = slice(t * P, (t + 1) * P)
             nc.tensor.matmul_mx(
-                out=b_ps[t // 2][:, t % 2, :], lhsT=w2_wd[:, t, :].bitcast(E5M2), lhsT_scale=w2_sd[:, t, :],
-                rhs=xo_wg[:].bitcast(E2M1), rhs_scale=xo_sg[:], start=True, stop=True,
+                out=b_ps[t // 2][:, t % 2, :], lhsT=w2_wd[:, cols].bitcast(E5M2), lhsT_scale=planes_b[:, J:][:, cols],
+                rhs=xo_wg[:].bitcast(E2M1), rhs_scale=planes_b[:, :J], start=True, stop=True,
             )
 
         gate = tile("gate", [P, PACK, J], F32)
         for t in range(PACK):
-            for u in range(2):
-                nc.scalar.activation(
-                    out=gate[:, t, u * 128 : (u + 1) * 128],
-                    in_=a_sb[t][:].indirect(l3[:, 8 * u : 8 * u + 8]),
-                    func=ACT.Sigmoid, bias=bg_t[:, t : t + 1], scale=sg_t[:, t : t + 1],
-                )
+            a_t = tile("a%d" % t, [P, 2 * J], F32)
+            nc.vector.tensor_copy(a_t[:, :J], a_ps[t][:])
+            nc.scalar.activation(
+                out=gate[:, t, :], in_=a_t[:].indirect(l3[:]),
+                func=ACT.Sigmoid, bias=bg_t[:, t : t + 1], scale=sg_t[:, t : t + 1],
+            )
 
         g4 = tile("g4", [P, PACK, O], F32)
         g5 = tile("g5", [P, PACK, O], F32)
@@ -154,27 +157,36 @@ def tile_list_gatedtwo_twotab_one_tabled_kernel(
             nc.vector.tensor_copy(g4[:, t, :], hg[:].indirect(l4[:]))
             nc.scalar.activation(out=g5[:, t, :], in_=hg[:].indirect(l5[:]), func=ACT.Copy)
 
-        tz_g = tile("tz_g", [P, 2, O], F32)
+        tz_g = tile("tz_g", [P, 2, O], F32, tag="gate")
         for h in range(2):
-            nc.scalar.activation(out=tz_g[:, h, :], in_=tz_t[:, h, :].indirect(l6[:]), func=ACT.Copy)
+            nc.scalar.activation(out=tz_g[:, h, :], in_=tz_sb[h][:].indirect(l6[:]), func=ACT.Copy)
 
         hid = tile("hid", [P, O * PACK], BF16)
-        nc.vector.tensor_tensor(
-            hid[:].rearrange("p (c i t) -> p c t i", i=4, t=PACK),
-            g4[:].rearrange("p t (c i) -> p c t i", i=4),
-            g5[:].rearrange("p t (c i) -> p c t i", i=4),
-            ALU.max,
-        )
         hid_w = tile("hid_w", [P, O], U32)
         hid_s = tile("hid_s", [P, O], U8)
-        nc.vector.quantize_mx(out=hid_w[:].bitcast(E4M3), scales=hid_s[:], in_=hid[:])
+        half = O // 2
+        for u in range(2):
+            cols = slice(u * half, (u + 1) * half)
+            nc.vector.tensor_tensor(
+                hid[:, u * half * PACK : (u + 1) * half * PACK].rearrange("p (c i t) -> p c t i", i=4, t=PACK),
+                g4[:, :, cols].rearrange("p t (c i) -> p c t i", i=4),
+                g5[:, :, cols].rearrange("p t (c i) -> p c t i", i=4),
+                ALU.max,
+            )
+        for u in range(2):
+            cols = slice(u * half, (u + 1) * half)
+            nc.vector.quantize_mx(
+                out=hid_w[:, cols].bitcast(E4M3), scales=hid_s[:, cols],
+                in_=hid[:, u * half * PACK : (u + 1) * half * PACK],
+            )
 
-        p_ps = ps.tile([P, 2, O], F32, name="p_ps")
         for h in range(2):
+            cols = slice(h * P, (h + 1) * P)
+            p_ps = ps.tile([P, O], F32, name="p_ps%d" % h)
             nc.tensor.matmul_mx(
-                out=p_ps[:, h, :], lhsT=wb_w[:, h * P : (h + 1) * P].bitcast(E5M2), lhsT_scale=wb_s[:, h * P : (h + 1) * P],
+                out=p_ps[:], lhsT=wb_w[:, cols].bitcast(E5M2), lhsT_scale=planes_b[:, J + R :][:, cols],
                 rhs=hid_w[:].bitcast(E4M3), rhs_scale=hid_s[:], start=True, stop=True,
             )
-        y = tile("y", [P, 2, O], F32)
-        nc.vector.tensor_tensor(y[:], p_ps[:], tz_g[:], ALU.add)
-        nc.sync.dma_start(out=out.rearrange("(h p) o -> p h o", p=P), in_=y[:])
+            y = tile("y%d" % h, [P, O], F32)
+            nc.vector.tensor_tensor(y[:], p_ps[:], tz_g[:, h, :], ALU.add)
+            (nc.sync, nc.scalar)[h].dma_start(out=out[cols, :], in_=y[:])

@@ -34,11 +34,11 @@ def deal_views(dealt, raw, run):
     )
 
 
-def spread_scale_rows(queue, planes):
-    for q in range(1, 4):
+def spread_scale_rows(queue, planes, rows, quadrants):
+    for q in quadrants:
         queue.dma_start(
             out=planes[32 * q : 32 * q + 4, :].bitcast(I32),
-            in_=planes[4 * q : 4 * q + 4, :].bitcast(I32),
+            in_=rows[4 * q : 4 * q + 4, :].bitcast(I32),
         )
 
 
@@ -66,51 +66,53 @@ def tile_list_gatedtwo_twotab_one_tabled_kernel(
         xo_w = tile("xo_w", [P, T], U16)
         xo_s = tile("xo_s", [P, T], U8)
         w_w = tile("w_w", [P, R], U16)
-        w2_w = tile("w2_w", [P, R], I32)
-        wb_w = tile("wb_w", [P, N], I32)
-        raw_s = tile("raw_s", [P, 2 * R], U8)
-        planes_a = tile("planes_a", [P, J + R], U8)
-        planes_b = tile("planes_b", [P, J + R + N], U8)
+        raw_s = tile("raw_s", [P, R], U8)
+        rows = tile("rows", [P, J + R + J], U8)
+        planes_a = rows[:, : J + R]
+        planes_b = tile("planes_b", [P, R + J], U8)
+        wb_s = tile("wb_s", [P, N], U8)
         sg_t = tile("sg_t", [P, PACK], F32)
         bg_t = tile("bg_t", [P, PACK], F32)
 
-        nc.gpsimd.memset(xt_s[:].bitcast(I32), 0)
-        nc.vector.memset(raw_s[:].bitcast(I32), 0)
+        nc.vector.memset(xt_s[:].bitcast(I32), 0)
         nc.vector.memset(xo_s[:].bitcast(I32), 0)
+        nc.vector.memset(raw_s[32:64, :].bitcast(I32), 0)
+        nc.vector.memset(raw_s[64:, :].bitcast(I32), 0)
 
         def load_rows(queue, dst, scales):
             queue.dma_start(out=dst.bitcast(I32), in_=scales[0].bitcast(I32))
 
         nc.sync.dma_start(l1[:], offs)
-        nc.sync.dma_start(out=wb_w[:], in_=wb_words[0].rearrange("p n t -> p (n t)").bitcast(I32))
-        load_rows(nc.sync, xt_s[:16, :], xt_scales)
-        load_rows(nc.sync, raw_s[:16, :R], w_scales)
+        load_rows(nc.sync, raw_s[:16, :], w_scales)
+        load_rows(nc.sync, raw_s[16:32, :], w2_scales)
         nc.sync.dma_start(l2[:], offs2)
-        load_rows(nc.sync, xo_s[:16, :], xo_scales)
-        load_rows(nc.sync, raw_s[:16, R:], w2_scales)
-        nc.sync.dma_start(out=xt_w[:], in_=xt_words[0].rearrange("p n t -> p (n t)").bitcast(I32))
-        load_rows(nc.gpsimd, planes_b[:16, J + R :], wb_scales)
-        nc.sync.dma_start(l3[:], offs3)
-        nc.sync.dma_start(out=sg_t[:], in_=sg.rearrange("(p t) o -> p (t o)", t=PACK))
-        nc.sync.dma_start(out=bg_t[:], in_=bg.rearrange("(p t) o -> p (t o)", t=PACK))
         nc.sync.dma_start(out=w_w[:].bitcast(I32), in_=w_words[0].bitcast(I32))
+        load_rows(nc.sync, xt_s[:16, :], xt_scales)
+        load_rows(nc.sync, xo_s[16:32, :], xo_scales)
+        nc.sync.dma_start(out=xt_w[:], in_=xt_words[0].rearrange("p n t -> p (n t)").bitcast(I32))
+        nc.gpsimd.dma_start(out=sg_t[:], in_=sg.rearrange("(p t) o -> p (t o)", t=PACK))
+        nc.gpsimd.dma_start(out=bg_t[:], in_=bg.rearrange("(p t) o -> p (t o)", t=PACK))
+        spread_scale_rows(nc.gpsimd, wb_s, wb_scales[0], range(4))
+        w2_w = tile("w2_w", [P, R], I32)
+        nc.sync.dma_start(l3[:], offs3)
         nc.sync.dma_start(out=xo_w[:].bitcast(I32), in_=xo_words[0].bitcast(I32))
         nc.sync.dma_start(out=w2_w[:], in_=w2_words[0].rearrange("p n t -> p (n t)").bitcast(I32))
-        nc.sync.dma_start(l4[:], offs4)
-        nc.sync.dma_start(l5[:], offs5)
-        nc.sync.dma_start(l6[:], offs6)
 
         xt_sg = tile("xt_sg", [P, J], U8)
+        nc.vector.tensor_copy(*deal_views(planes_a[:, J:], raw_s[:], LINE))
         nc.vector.tensor_copy(xt_sg[:], xt_s[:].indirect(l1[:]))
-        nc.vector.tensor_copy(*deal_views(planes_a[:, J:], raw_s[:, :R], LINE))
         nc.vector.tensor_copy(planes_a[:, :J].bitcast(I32), xt_sg[:].bitcast(I32))
-        spread_scale_rows(nc.sync, planes_a)
+        spread_scale_rows(nc.sync, planes_a, planes_a, range(1, 4))
 
         xo_sg = tile("xo_sg", [P, J], U8)
         nc.vector.tensor_copy(xo_sg[:], xo_s[:].indirect(l2[:]))
-        nc.vector.tensor_copy(*deal_views(planes_b[:, J : J + R], raw_s[:, R:], LINE))
-        nc.vector.tensor_copy(planes_b[:, :J].bitcast(I32), xo_sg[:].bitcast(I32))
-        spread_scale_rows(nc.sync, planes_b)
+        nc.vector.tensor_copy(rows[:, J + R :].bitcast(I32), xo_sg[:].bitcast(I32))
+        spread_scale_rows(nc.sync, planes_b, rows[16:32, J:], range(4))
+        nc.sync.dma_start(l4[:], offs4)
+        nc.sync.dma_start(l5[:], offs5)
+        nc.sync.dma_start(l6[:], offs6)
+        wb_w = tile("wb_w", [P, N], I32, tag="xo_sg")
+        nc.sync.dma_start(out=wb_w[:], in_=wb_words[0].rearrange("p n t -> p (n t)").bitcast(I32))
 
         xt_wg = tile("xt_wg", [P, J], U32)
         w_wd = tile("w_wd", [P, R], U16)
@@ -121,7 +123,7 @@ def tile_list_gatedtwo_twotab_one_tabled_kernel(
         nc.vector.tensor_copy(xo_wg[:], xo_w[:].indirect(l2[:]))
         nc.vector.tensor_copy(*deal_views(w2_wd[:], w2_w[:], LINE // 4))
 
-        tz_sb = [tile("tz%d" % h, [P, E], F32, tag=("xo_w", "w2_w")[h]) for h in range(2)]
+        tz_sb = [tile("tz%d" % h, [P, E], F32, tag=("xt_w", "xo_w")[h]) for h in range(2)]
         for h in range(2):
             nc.sync.dma_start(out=tz_sb[h][:], in_=tz[h * P : (h + 1) * P, :])
 
@@ -132,12 +134,12 @@ def tile_list_gatedtwo_twotab_one_tabled_kernel(
                 out=a_ps[t][:], lhsT=w_wd[:, cols].bitcast(E2M1), lhsT_scale=planes_a[:, J:][:, cols],
                 rhs=xt_wg[:].bitcast(E4M3), rhs_scale=planes_a[:, :J], start=True, stop=True,
             )
-        b_ps = [ps.tile([P, 2, J], F32, name="b_ps%d" % u) for u in range(2)]
+        b_ps = [ps.tile([P, J], F32, name="b_ps%d" % t) for t in range(PACK)]
         for t in range(PACK):
             cols = slice(t * P, (t + 1) * P)
             nc.tensor.matmul_mx(
-                out=b_ps[t // 2][:, t % 2, :], lhsT=w2_wd[:, cols].bitcast(E5M2), lhsT_scale=planes_b[:, J:][:, cols],
-                rhs=xo_wg[:].bitcast(E2M1), rhs_scale=planes_b[:, :J], start=True, stop=True,
+                out=b_ps[t][:], lhsT=w2_wd[:, cols].bitcast(E5M2), lhsT_scale=planes_b[:, cols],
+                rhs=xo_wg[:].bitcast(E2M1), rhs_scale=planes_b[:, R:], start=True, stop=True,
             )
 
         gate = tile("gate", [P, PACK, J], F32)
@@ -153,9 +155,13 @@ def tile_list_gatedtwo_twotab_one_tabled_kernel(
         g5 = tile("g5", [P, PACK, O], F32)
         for t in range(PACK):
             hg = tile("hg%d" % t, [P, J], F32)
-            nc.vector.tensor_tensor(hg[:], gate[:, t, :], b_ps[t // 2][:, t % 2, :], ALU.mult)
+            nc.vector.tensor_tensor(hg[:], gate[:, t, :], b_ps[t][:], ALU.mult)
             nc.vector.tensor_copy(g4[:, t, :], hg[:].indirect(l4[:]))
-            nc.scalar.activation(out=g5[:, t, :], in_=hg[:].indirect(l5[:]), func=ACT.Copy)
+            if t < PACK - 1:
+                nc.scalar.activation(out=g5[:, t, :], in_=hg[:].indirect(l5[:]), func=ACT.Copy)
+            else:
+                nc.scalar.activation(out=g5[:, t, :64], in_=hg[:].indirect(l5[:, :4]), func=ACT.Copy)
+                nc.vector.tensor_copy(g5[:, t, 64:], hg[:].indirect(l5[:, 4:]))
 
         tz_g = tile("tz_g", [P, 2, O], F32, tag="gate")
         for h in range(2):
@@ -182,9 +188,9 @@ def tile_list_gatedtwo_twotab_one_tabled_kernel(
 
         for h in range(2):
             cols = slice(h * P, (h + 1) * P)
-            p_ps = ps.tile([P, O], F32, name="p_ps%d" % h)
+            p_ps = ps.tile([P, O], F32, name="p_ps%d" % h, tag="a_ps%d" % h)
             nc.tensor.matmul_mx(
-                out=p_ps[:], lhsT=wb_w[:, cols].bitcast(E5M2), lhsT_scale=planes_b[:, J + R :][:, cols],
+                out=p_ps[:], lhsT=wb_w[:, cols].bitcast(E5M2), lhsT_scale=wb_s[:, cols],
                 rhs=hid_w[:].bitcast(E4M3), rhs_scale=hid_s[:], start=True, stop=True,
             )
             y = tile("y%d" % h, [P, O], F32)

@@ -67,10 +67,10 @@ def tile_list_gatedtwo_twotab_one_tabled_kernel(
         xo_s = tile("xo_s", [P, T], U8)
         w_w = tile("w_w", [P, R], U16)
         raw_s = tile("raw_s", [P, R], U8)
-        rows = tile("rows", [P, J + R + J], U8)
+        rows = tile("rows", [P, J + R + J + N], U8)
         planes_a = rows[:, : J + R]
-        planes_b = tile("planes_b", [P, R + J], U8)
-        wb_s = tile("wb_s", [P, N], U8)
+        planes_b = tile("planes_b", [P, R + J + N], U8)
+        wb_s = planes_b[:, R + J :]
         sg_t = tile("sg_t", [P, PACK], F32)
         bg_t = tile("bg_t", [P, PACK], F32)
 
@@ -79,12 +79,16 @@ def tile_list_gatedtwo_twotab_one_tabled_kernel(
         nc.vector.memset(raw_s[32:64, :].bitcast(I32), 0)
         nc.vector.memset(raw_s[64:, :].bitcast(I32), 0)
 
+        warm = tile("warm", [P, 2], F32)
+        nc.gpsimd.memset(warm[:, 0:1], 0.0)
+        nc.scalar.activation(out=warm[:, 1:2], in_=warm[:, 0:1], func=ACT.Sigmoid)
+
         def load_rows(queue, dst, scales):
             queue.dma_start(out=dst.bitcast(I32), in_=scales[0].bitcast(I32))
 
-        nc.sync.dma_start(l1[:], offs)
         load_rows(nc.sync, raw_s[:16, :], w_scales)
         load_rows(nc.sync, raw_s[16:32, :], w2_scales)
+        nc.sync.dma_start(l1[:], offs)
         nc.sync.dma_start(l2[:], offs2)
         nc.sync.dma_start(out=w_w[:].bitcast(I32), in_=w_words[0].bitcast(I32))
         load_rows(nc.sync, xt_s[:16, :], xt_scales)
@@ -92,9 +96,9 @@ def tile_list_gatedtwo_twotab_one_tabled_kernel(
         nc.sync.dma_start(out=xt_w[:], in_=xt_words[0].rearrange("p n t -> p (n t)").bitcast(I32))
         nc.gpsimd.dma_start(out=sg_t[:], in_=sg.rearrange("(p t) o -> p (t o)", t=PACK))
         nc.gpsimd.dma_start(out=bg_t[:], in_=bg.rearrange("(p t) o -> p (t o)", t=PACK))
-        spread_scale_rows(nc.gpsimd, wb_s, wb_scales[0], range(4))
         w2_w = tile("w2_w", [P, R], I32)
         nc.sync.dma_start(l3[:], offs3)
+        load_rows(nc.sync, rows[16:32, J + R + J :], wb_scales)
         nc.sync.dma_start(out=xo_w[:].bitcast(I32), in_=xo_words[0].bitcast(I32))
         nc.sync.dma_start(out=w2_w[:], in_=w2_words[0].rearrange("p n t -> p (n t)").bitcast(I32))
 
@@ -106,7 +110,7 @@ def tile_list_gatedtwo_twotab_one_tabled_kernel(
 
         xo_sg = tile("xo_sg", [P, J], U8)
         nc.vector.tensor_copy(xo_sg[:], xo_s[:].indirect(l2[:]))
-        nc.vector.tensor_copy(rows[:, J + R :].bitcast(I32), xo_sg[:].bitcast(I32))
+        nc.vector.tensor_copy(rows[:, J + R : J + R + J].bitcast(I32), xo_sg[:].bitcast(I32))
         spread_scale_rows(nc.sync, planes_b, rows[16:32, J:], range(4))
         nc.sync.dma_start(l4[:], offs4)
         nc.sync.dma_start(l5[:], offs5)
@@ -117,11 +121,11 @@ def tile_list_gatedtwo_twotab_one_tabled_kernel(
         xt_wg = tile("xt_wg", [P, J], U32)
         w_wd = tile("w_wd", [P, R], U16)
         nc.vector.tensor_copy(xt_wg[:], xt_w[:].bitcast(U32).indirect(l1[:]))
-        nc.vector.tensor_copy(*deal_views(w_wd[:], w_w[:], LINE // 2))
+        nc.scalar.copy(*deal_views(w_wd[:], w_w[:], LINE // 2))
         xo_wg = tile("xo_wg", [P, J], U16)
-        w2_wd = tile("w2_wd", [P, R], I32)
+        w2_wd = tile("w2_wd", [P, R], U32)
         nc.vector.tensor_copy(xo_wg[:], xo_w[:].indirect(l2[:]))
-        nc.vector.tensor_copy(*deal_views(w2_wd[:], w2_w[:], LINE // 4))
+        nc.scalar.copy(*deal_views(w2_wd[:], w2_w[:].bitcast(U32), LINE // 4))
 
         tz_sb = [tile("tz%d" % h, [P, E], F32, tag=("xt_w", "xo_w")[h]) for h in range(2)]
         for h in range(2):
@@ -139,13 +143,16 @@ def tile_list_gatedtwo_twotab_one_tabled_kernel(
             cols = slice(t * P, (t + 1) * P)
             nc.tensor.matmul_mx(
                 out=b_ps[t][:], lhsT=w2_wd[:, cols].bitcast(E5M2), lhsT_scale=planes_b[:, cols],
-                rhs=xo_wg[:].bitcast(E2M1), rhs_scale=planes_b[:, R:], start=True, stop=True,
+                rhs=xo_wg[:].bitcast(E2M1), rhs_scale=planes_b[:, R : R + J], start=True, stop=True,
             )
 
         gate = tile("gate", [P, PACK, J], F32)
         for t in range(PACK):
             a_t = tile("a%d" % t, [P, 2 * J], F32)
-            nc.vector.tensor_copy(a_t[:, :J], a_ps[t][:])
+            if t == 0:
+                nc.scalar.copy(a_t[:, :J], a_ps[t][:])
+            else:
+                nc.vector.tensor_copy(a_t[:, :J], a_ps[t][:])
             nc.scalar.activation(
                 out=gate[:, t, :], in_=a_t[:].indirect(l3[:]),
                 func=ACT.Sigmoid, bias=bg_t[:, t : t + 1], scale=sg_t[:, t : t + 1],

from contextlib import ExitStack

import concourse.mybir as mybir

FLOPS = 301989888

F32 = mybir.dt.float32
BF16 = mybir.dt.bfloat16
I32 = mybir.dt.int32
U32 = mybir.dt.uint32
U16 = mybir.dt.uint16
U8 = mybir.dt.uint8
E4M3 = mybir.dt.float8_e4m3fn_x4
E5M2 = mybir.dt.float8_e5m2_x4
E2M1 = mybir.dt.float4_e2m1fn_x4
ACT = mybir.ActivationFunctionType
ALU = mybir.AluOpType

P = 128
PACK = 4
T = 1024
J = 256
R = 512
O = 128
N = 256
E = 1024
LINE = 16


def deal_views(dealt, raw, run):
    return (
        dealt.rearrange("p (t c i) -> p c t i", i=run, t=PACK),
        raw.rearrange("p (c i t) -> p c t i", i=run, t=PACK),
    )


def spread_scale_rows(queue, planes, rows, quadrants):
    for q in quadrants:
        queue.dma_start(
            out=planes[32 * q : 32 * q + 4, :].bitcast(I32),
            in_=rows[4 * q : 4 * q + 4, :].bitcast(I32),
        )


def tile_list_gatedtwo_twotab_one_tabled_kernel(
    tc, xt_words, xt_scales, w_words, w_scales, xo_words, xo_scales, w2_words, w2_scales,
    sg, bg, wb_words, wb_scales, tz, offs, offs2, offs3, offs4, offs5, offs6, out,
):
    nc = tc.nc
    with ExitStack() as ctx:
        sb = ctx.enter_context(tc.tile_pool(name="sb", bufs=1))
        ps = ctx.enter_context(tc.psum_pool(name="ps", bufs=1))

        def tile(name, shape, dtype, tag=None):
            return sb.tile(shape, dtype, name=name, tag=tag or name, align_bytes=64)

        l1 = tile("l1", [P, J // 16], U16)
        l2 = tile("l2", [P, J // 16], U16)
        l3 = tile("l3", [P, J // 16], U16)
        l4 = tile("l4", [P, O // 16], U16)
        l5 = tile("l5", [P, O // 16], U16)
        l6 = tile("l6", [P, O // 16], U16)

        xt_w = tile("xt_w", [P, T], I32)
        xt_s = tile("xt_s", [P, T], U8)
        xo_w = tile("xo_w", [P, T], U16)
        xo_s = tile("xo_s", [P, T], U8)
        w_w = tile("w_w", [P, R], U16)
        raw_s = tile("raw_s", [P, R], U8)
        rows = tile("rows", [P, J + R + J + N], U8)
        planes_a = rows[:, : J + R]
        planes_b = tile("planes_b", [P, R + J + N], U8)
        wb_s = planes_b[:, R + J :]
        sg_t = tile("sg_t", [P, PACK], F32)
        bg_t = tile("bg_t", [P, PACK], F32)

        nc.vector.memset(xt_s[:].bitcast(I32), 0)
        nc.vector.memset(xo_s[:].bitcast(I32), 0)
        nc.vector.memset(raw_s[32:64, :].bitcast(I32), 0)
        nc.vector.memset(raw_s[64:, :].bitcast(I32), 0)

        warm = tile("warm", [P, 2], F32)
        nc.gpsimd.memset(warm[:, 0:1], 0.0)
        nc.scalar.activation(out=warm[:, 1:2], in_=warm[:, 0:1], func=ACT.Sigmoid)

        def load_rows(queue, dst, scales):
            queue.dma_start(out=dst.bitcast(I32), in_=scales[0].bitcast(I32))

        load_rows(nc.sync, raw_s[:16, :], w_scales)
        load_rows(nc.sync, raw_s[16:32, :], w2_scales)
        nc.sync.dma_start(l1[:], offs)
        nc.sync.dma_start(l2[:], offs2)
        nc.sync.dma_start(out=w_w[:].bitcast(I32), in_=w_words[0].bitcast(I32))
        load_rows(nc.sync, xt_s[:16, :], xt_scales)
        load_rows(nc.sync, xo_s[16:32, :], xo_scales)
        nc.sync.dma_start(out=xt_w[:], in_=xt_words[0].rearrange("p n t -> p (n t)").bitcast(I32))
        nc.gpsimd.dma_start(out=sg_t[:], in_=sg.rearrange("(p t) o -> p (t o)", t=PACK))
        nc.gpsimd.dma_start(out=bg_t[:], in_=bg.rearrange("(p t) o -> p (t o)", t=PACK))
        w2_w = tile("w2_w", [P, R], I32)
        nc.sync.dma_start(l3[:], offs3)
        load_rows(nc.sync, rows[16:32, J + R + J :], wb_scales)
        nc.sync.dma_start(out=xo_w[:].bitcast(I32), in_=xo_words[0].bitcast(I32))
        nc.sync.dma_start(out=w2_w[:], in_=w2_words[0].rearrange("p n t -> p (n t)").bitcast(I32))

        xt_sg = tile("xt_sg", [P, J], U8)
        nc.vector.tensor_copy(*deal_views(planes_a[:, J:], raw_s[:], LINE))
        nc.vector.tensor_copy(xt_sg[:], xt_s[:].indirect(l1[:]))
        nc.vector.tensor_copy(planes_a[:, :J].bitcast(I32), xt_sg[:].bitcast(I32))
        spread_scale_rows(nc.sync, planes_a, planes_a, range(1, 4))

        xo_sg = tile("xo_sg", [P, J], U8)
        nc.vector.tensor_copy(xo_sg[:], xo_s[:].indirect(l2[:]))
        nc.vector.tensor_copy(rows[:, J + R : J + R + J].bitcast(I32), xo_sg[:].bitcast(I32))
        spread_scale_rows(nc.sync, planes_b, rows[16:32, J:], range(4))
        nc.sync.dma_start(l4[:], offs4)
        nc.sync.dma_start(l5[:], offs5)
        nc.sync.dma_start(l6[:], offs6)
        wb_w = tile("wb_w", [P, N], I32, tag="xo_sg")
        nc.sync.dma_start(out=wb_w[:], in_=wb_words[0].rearrange("p n t -> p (n t)").bitcast(I32))

        xt_wg = tile("xt_wg", [P, J], U32)
        w_wd = tile("w_wd", [P, R], U16)
        nc.vector.tensor_copy(xt_wg[:], xt_w[:].bitcast(U32).indirect(l1[:]))
        nc.scalar.copy(*deal_views(w_wd[:], w_w[:], LINE // 2))
        xo_wg = tile("xo_wg", [P, J], U16)
        w2_wd = tile("w2_wd", [P, R], U32)
        nc.vector.tensor_copy(xo_wg[:], xo_w[:].indirect(l2[:]))
        nc.scalar.copy(*deal_views(w2_wd[:], w2_w[:].bitcast(U32), LINE // 4))

        tz_sb = [tile("tz%d" % h, [P, E], F32, tag=("xt_w", "xo_w")[h]) for h in range(2)]
        for h in range(2):
            nc.sync.dma_start(out=tz_sb[h][:], in_=tz[h * P : (h + 1) * P, :])

        a_ps = [ps.tile([P, J], F32, name="a_ps%d" % t) for t in range(PACK)]
        for t in range(PACK):
            cols = slice(t * P, (t + 1) * P)
            nc.tensor.matmul_mx(
                out=a_ps[t][:], lhsT=w_wd[:, cols].bitcast(E2M1), lhsT_scale=planes_a[:, J:][:, cols],
                rhs=xt_wg[:].bitcast(E4M3), rhs_scale=planes_a[:, :J], start=True, stop=True,
            )
        b_ps = [ps.tile([P, J], F32, name="b_ps%d" % t) for t in range(PACK)]
        for t in range(PACK):
            cols = slice(t * P, (t + 1) * P)
            nc.tensor.matmul_mx(
                out=b_ps[t][:], lhsT=w2_wd[:, cols].bitcast(E5M2), lhsT_scale=planes_b[:, cols],
                rhs=xo_wg[:].bitcast(E2M1), rhs_scale=planes_b[:, R : R + J], start=True, stop=True,
            )

        gate = tile("gate", [P, PACK, J], F32)
        for t in range(PACK):
            a_t = tile("a%d" % t, [P, 2 * J], F32)
            if t == 0:
                nc.scalar.copy(a_t[:, :J], a_ps[t][:])
            else:
                nc.vector.tensor_copy(a_t[:, :J], a_ps[t][:])
            nc.scalar.activation(
                out=gate[:, t, :], in_=a_t[:].indirect(l3[:]),
                func=ACT.Sigmoid, bias=bg_t[:, t : t + 1], scale=sg_t[:, t : t + 1],
            )

        g4 = tile("g4", [P, PACK, O], F32)
        g5 = tile("g5", [P, PACK, O], F32)
        for t in range(PACK):
            hg = tile("hg%d" % t, [P, J], F32)
            nc.vector.tensor_tensor(hg[:], gate[:, t, :], b_ps[t][:], ALU.mult)
            nc.vector.tensor_copy(g4[:, t, :], hg[:].indirect(l4[:]))
            if t < PACK - 1:
                nc.scalar.activation(out=g5[:, t, :], in_=hg[:].indirect(l5[:]), func=ACT.Copy)
            else:
                nc.scalar.activation(out=g5[:, t, :64], in_=hg[:].indirect(l5[:, :4]), func=ACT.Copy)
                nc.vector.tensor_copy(g5[:, t, 64:], hg[:].indirect(l5[:, 4:]))

        tz_g = tile("tz_g", [P, 2, O], F32, tag="gate")
        for h in range(2):
            nc.scalar.activation(out=tz_g[:, h, :], in_=tz_sb[h][:].indirect(l6[:]), func=ACT.Copy)

        hid = tile("hid", [P, O * PACK], BF16)
        hid_w = tile("hid_w", [P, O], U32)
        hid_s = tile("hid_s", [P, O], U8)
        half = O // 2
        for u in range(2):
            cols = slice(u * half, (u + 1) * half)
            nc.vector.tensor_tensor(
                hid[:, u * half * PACK : (u + 1) * half * PACK].rearrange("p (c i t) -> p c t i", i=4, t=PACK),
                g4[:, :, cols].rearrange("p t (c i) -> p c t i", i=4),
                g5[:, :, cols].rearrange("p t (c i) -> p c t i", i=4),
                ALU.max,
            )
        for u in range(2):
            cols = slice(u * half, (u + 1) * half)
            nc.vector.quantize_mx(
                out=hid_w[:, cols].bitcast(E4M3), scales=hid_s[:, cols],
                in_=hid[:, u * half * PACK : (u + 1) * half * PACK],
            )

        for h in range(2):
            cols = slice(h * P, (h + 1) * P)
            p_ps = ps.tile([P, O], F32, name="p_ps%d" % h, tag="a_ps%d" % h)
            nc.tensor.matmul_mx(
                out=p_ps[:], lhsT=wb_w[:, cols].bitcast(E5M2), lhsT_scale=wb_s[:, cols],
                rhs=hid_w[:].bitcast(E4M3), rhs_scale=hid_s[:], start=True, stop=True,
            )
            y = tile("y%d" % h, [P, O], F32)
            nc.vector.tensor_tensor(y[:], p_ps[:], tz_g[:, h, :], ALU.add)
            (nc.sync, nc.scalar)[h].dma_start(out=out[cols, :], in_=y[:])
